import numpy as np
import ml_dtypes


def mxq(x, axis, fmt="e4m3"):
    dtype, down = {"e4m3": (ml_dtypes.float8_e4m3fn, 7), "e5m2": (ml_dtypes.float8_e5m2, 14)}[fmt]
    v = np.moveaxis(np.asarray(x, np.float32).astype(ml_dtypes.bfloat16).astype(np.float64), axis, -1)
    blocks = v.reshape(v.shape[:-1] + (-1, 32))
    amax = np.abs(blocks).max(-1, keepdims=True)
    byte = np.maximum(np.where(amax > 0, np.frexp(amax)[1] - 1 + 127, 0) - down, 1)
    scale = np.exp2(byte - 127.0)
    codes = (blocks / scale).astype(np.float32).astype(dtype).astype(np.float64)
    return np.moveaxis((codes * scale).reshape(v.shape), -1, axis)


WIDE = False


def mx_kscale(k):
    if not WIDE:
        return np.ones(k)
    levels = np.array([10, -10, 5, -5, 0])
    if k % 512:
        return np.exp2(np.random.permutation(np.resize(levels, k // 32))).repeat(32)
    a = np.empty((k // 512, 16))
    for p in range(k // 512):
        a[p, :8] = np.random.permutation(np.resize(levels, 8))
        for g in range(8):
            far = levels[np.abs(levels - a[p, g]) >= 10]
            a[p, g + 8] = far[np.random.randint(len(far))]
    return np.exp2(a.ravel()).repeat(32)


def f64(x):
    return np.asarray(x).astype(np.float64)


def striped(idx):
    return np.tile(idx.reshape(-1, 16).T, (8, 1)).astype(np.uint16)


def unstriped(offs):
    return offs[:16].T.reshape(-1).astype(np.int64)


def pack_weight(w):
    k, n = w.shape
    w = f64(np.asarray(w, np.float32).astype(ml_dtypes.bfloat16)).reshape(k // 32, 32, n)
    amax = np.abs(w).max(1)
    byte = np.clip(np.where(amax > 0, np.frexp(amax)[1] - 1 + 127 - 7, 1), 1, 254)
    scaled = (w * np.exp2(127.0 - byte)[:, None, :]).reshape(k, n).astype(np.float32)
    words = np.ascontiguousarray(scaled.reshape(k // 512, 128, 4, n).transpose(0, 1, 3, 2)).astype(ml_dtypes.float8_e4m3fn).view(np.uint8)
    return words, np.ascontiguousarray(byte.astype(np.uint8).reshape(k // 512, 16, n))


def unpack_weight(words, scales):
    g, p, n, _ = words.shape
    vals = np.ascontiguousarray(words).view(ml_dtypes.float8_e4m3fn).astype(np.float64) * np.repeat(np.exp2(scales.astype(np.float64) - 127.0), 8, axis=1)[..., None]
    return vals.transpose(0, 1, 3, 2).reshape(g * 512, n)


E2M1 = np.array([0.0, 0.5, 1.0, 1.5, 2.0, 3.0, 4.0, 6.0, -0.0, -0.5, -1.0, -1.5, -2.0, -3.0, -4.0, -6.0])


def pack_fp4(w):
    k, n = w.shape
    w = f64(np.asarray(w, np.float32).astype(ml_dtypes.bfloat16)).reshape(k // 32, 32, n)
    amax = np.abs(w).max(1)
    mant, ex = np.frexp(amax / 6.0)
    byte = np.clip(np.where(amax > 0, np.where(mant > 0.5, ex, ex - 1) + 127, 1), 1, 254)
    scaled = (w * np.exp2(127.0 - byte)[:, None, :]).reshape(k, n).astype(np.float32)
    c = np.ascontiguousarray(scaled.reshape(k // 512, 128, 4, n).transpose(0, 1, 3, 2)).astype(ml_dtypes.float4_e2m1fn).view(np.uint8) & 0xF
    words = (c[..., 0::2] | (c[..., 1::2] << 4)).reshape(k // 512, 128, 2 * n)
    return np.ascontiguousarray(words), np.ascontiguousarray(byte.astype(np.uint8).reshape(k // 512, 16, n))


def unpack_fp4(words, scales):
    g, _, n = scales.shape
    words = np.ascontiguousarray(words).reshape(g, 128, n, 2)
    nib = np.empty((g, 128, n, 4), np.uint8)
    nib[..., 0::2] = words & 0xF
    nib[..., 1::2] = words >> 4
    vals = E2M1[nib] * np.repeat(np.exp2(scales.astype(np.float64) - 127.0), 8, axis=1)[..., None]
    return vals.transpose(0, 1, 3, 2).reshape(g * 512, n)


K, T, S, N, H = 512, 1024, 512, 128, 512


def setup_inputs():
    n = np.random.standard_normal
    s = mx_kscale(K)[:, None]
    u = mx_kscale(H)
    packed_xT = pack_weight(n((K, T)) * s)
    packed_w1 = pack_fp4(n((K, H)) / np.sqrt(K) / s)
    packed_w2 = pack_fp4(n((K, H)) / np.sqrt(K) / s)
    packed_w3 = pack_fp4(n((H, N)) / np.sqrt(H) / u[:, None])
    return {
        "x_words": packed_xT[0],
        "x_scales": packed_xT[1],
        "w1_words": packed_w1[0],
        "w1_scales": packed_w1[1],
        "w2_words": packed_w2[0],
        "w2_scales": packed_w2[1],
        "ra": (n((H, S))).astype(np.float32),
        "rb": (n((H, S))).astype(np.float32),
        "unit": (np.random.uniform(0.6, 1.4, (H, 1)) * u[:, None]).astype(np.float32),
        "w3_words": packed_w3[0],
        "w3_scales": packed_w3[1],
        "offs": striped(np.random.permutation(T)[:S]),
        "ant": striped(np.random.permutation(S)),
    }


def reference(x_words, x_scales, w1_words, w1_scales, w2_words, w2_scales, ra, rb, unit, w3_words, w3_scales, offs, ant):
    xq = unpack_weight(x_words, x_scales)[:, unstriped(offs)]
    hr = unpack_fp4(w1_words, w1_scales).T @ xq
    hi2 = unpack_fp4(w2_words, w2_scales).T @ xq
    gr = hr[:, unstriped(ant)]
    gi = hi2[:, unstriped(ant)]
    en = (hr) ** 2 + (hi2) ** 2 + (gr) ** 2 + (gi) ** 2 + 0.3
    sym1 = (hr * f64(ra) + gr * f64(rb) + 0.5 * (hi2 * f64(rb))) / en
    llr = (0.5 * np.sqrt(en)) * sym1
    sym2 = (gi * f64(ra) - (hi2 * f64(rb))) / en
    hid = f64(unit) * (np.tanh(llr) * en - sym2[:, unstriped(ant)])
    return unpack_fp4(w3_words, w3_scales).T @ mxq(hid, 0, "e4m3")

@@ -1,0 +1,213 @@
+from contextlib import ExitStack
+
+import concourse.mybir as mybir
+from concourse.masks import make_identity
+
+K, T, S, N, H = 512, 1024, 512, 128, 512
+FLOPS = 2 * K * S * H * 2 + 2 * H * S * N
+
+F32 = mybir.dt.float32
+BF16 = mybir.dt.bfloat16
+I32 = mybir.dt.int32
+U32 = mybir.dt.uint32
+U16 = mybir.dt.uint16
+U8 = mybir.dt.uint8
+FP8X4 = mybir.dt.float8_e4m3fn_x4
+FP4X4 = mybir.dt.float4_e2m1fn_x4
+ACT = mybir.ActivationFunctionType
+MULT = mybir.AluOpType.mult
+ADD = mybir.AluOpType.add
+
+P = 128
+PACK = 4
+HALF = S // 2
+
+
+def load_scale_rows(nc, queue, plane, scales):
+    for q in range(4):
+        rows = scales[0, 4 * q : 4 * q + 4, :].bitcast(I32)
+        queue.dma_start(out=plane[32 * q : 32 * q + 32, :].bitcast(I32), in_=rows.partition_broadcast(8))
+
+
+def tile_picked_yalamo_tanh_p_kernel(
+    tc, x_words, x_scales, w1_words, w1_scales, w2_words, w2_scales, ra, rb, unit, w3_words, w3_scales, offs, ant, out
+):
+    nc = tc.nc
+    with ExitStack() as ctx:
+        sb = ctx.enter_context(tc.tile_pool(name="sb", bufs=1))
+        psum = ctx.enter_context(tc.psum_pool(name="psum", bufs=1))
+
+        def plane(name, width=S, dtype=F32):
+            return sb.tile([P, width], dtype, name=name, align_bytes=64)
+
+        offs_t = sb.tile([P, S // 16], U16, name="offs_t")
+        ant_t = sb.tile([P, S // 16], U16, name="ant_t")
+        xw = plane("xw", T, U32)
+        xs = plane("xs", T, U8)
+        w_raw = [plane("w_raw%d" % i, 2 * H, U8) for i in range(2)]
+        ws_raw = [plane("ws_raw%d" % i, H, U8) for i in range(2)]
+        w3w = plane("w3w", 2 * N, U8)
+        w3s = plane("w3s", N, U8)
+        ra_t = [plane("ra%d" % t) for t in range(PACK)]
+        rb_t = [plane("rb%d" % t) for t in range(PACK)]
+        unit_t = plane("unit_t", PACK)
+
+        ident = plane("ident", P)
+
+        nc.sync.dma_start(out=w_raw[0][:].bitcast(I32), in_=w1_words[0].bitcast(I32))
+        nc.sync.dma_start(out=w_raw[1][:].bitcast(I32), in_=w2_words[0].bitcast(I32))
+        nc.sync.dma_start(offs_t[:], offs)
+        nc.sync.dma_start(out=xw[:].bitcast(I32), in_=x_words[0].rearrange("p n r -> p (n r)").bitcast(I32))
+        load_scale_rows(nc, nc.sync, xs, x_scales)
+        load_scale_rows(nc, nc.sync, ws_raw[0], w1_scales)
+        load_scale_rows(nc, nc.sync, ws_raw[1], w2_scales)
+        make_identity(nc, ident[:])
+        nc.sync.dma_start(ant_t[:], ant)
+        ra_v = ra.rearrange("(p t) s -> p t s", t=PACK)
+        rb_v = rb.rearrange("(p t) s -> p t s", t=PACK)
+        for t in range(PACK):
+            nc.sync.dma_start(out=rb_t[t][:], in_=rb_v[:, t, :])
+            nc.sync.dma_start(out=ra_t[t][:], in_=ra_v[:, t, :])
+        nc.sync.dma_start(out=unit_t[:], in_=unit.rearrange("(p t) o -> p (t o)", t=PACK))
+        nc.sync.dma_start(out=w3w[:].bitcast(I32), in_=w3_words[0].bitcast(I32))
+        load_scale_rows(nc, nc.sync, w3s, w3_scales)
+
+        w_dealt = [plane("w_dealt%d" % i, 2 * H, U8) for i in range(2)]
+        ws_dealt = [plane("ws_dealt%d" % i, H, U8) for i in range(2)]
+        xg = plane("xg", S, U32)
+        xsg = plane("xsg", S, U8)
+        for i in range(2):
+            nc.vector.tensor_copy(
+                w_dealt[i][:].rearrange("p (t m b) -> p t m b", t=PACK, b=2),
+                w_raw[i][:].rearrange("p (m t b) -> p t m b", t=PACK, b=2),
+            )
+        nc.vector.tensor_copy(xg[:], xw[:].indirect(offs_t[:]))
+        nc.vector.tensor_copy(xsg[:], xs[:].indirect(offs_t[:]))
+        for i in range(2):
+            nc.vector.tensor_copy(
+                ws_dealt[i][:].rearrange("p (t m) -> p t m", t=PACK),
+                ws_raw[i][:].rearrange("p (m t) -> p t m", t=PACK),
+            )
+
+        def bank_tile(index, name):
+            return psum.tile([P, S], F32, name=name, tag="bank%d" % index)
+
+        def turn(bank, cols, src, start, stop):
+            nc.tensor.matmul(bank[:, cols], src, ident[:], start=start, stop=stop, is_transpose=True)
+
+        def turn_and_add(bank, terms):
+            for n, term in enumerate(terms):
+                for jb in range(PACK):
+                    cols = slice(jb * P, (jb + 1) * P)
+                    turn(bank, cols, term[:, cols], n == 0 and jb == 0, n == len(terms) - 1 and jb == PACK - 1)
+
+        a_win = [plane("a_win%d" % t, 2 * S) for t in range(PACK)]
+        b_win = [plane("b_win%d" % t, 2 * S) for t in range(PACK)]
+        p_win = [plane("p_win%d" % t, 2 * S) for t in range(PACK)]
+        s_win = [plane("s_win%d" % t) for t in range(PACK)]
+        ara = [plane("ara%d" % t) for t in range(PACK)]
+        crb = [plane("crb%d" % t) for t in range(PACK)]
+        pg = [plane("pg%d" % t) for t in range(PACK)]
+        y = [plane("y%d" % t) for t in range(PACK)]
+        rs = [plane("rs%d" % t) for t in range(PACK)]
+        inv = [plane("inv%d" % t) for t in range(PACK)]
+        llr = sb.tile([P, PACK, S], F32, name="llr", align_bytes=64)
+        sg = [sb.tile([P, PACK, HALF], F32, name="sg%d" % h, align_bytes=64) for h in range(2)]
+
+        products = []
+        for t in range(PACK):
+            for i in range(2):
+                bank = bank_tile(2 * t + i, "prod%d" % (2 * t + i))
+                nc.tensor.matmul_mx(
+                    out=bank[:],
+                    lhsT=w_dealt[i][:, 2 * P * t : 2 * P * (t + 1)].bitcast(FP4X4),
+                    lhsT_scale=ws_dealt[i][:, P * t : P * (t + 1)],
+                    rhs=xg[:].bitcast(FP8X4),
+                    rhs_scale=xsg[:],
+                    start=True,
+                    stop=True,
+                )
+                products.append(bank)
+
+        en_turned = {}
+        n1_turned = {}
+
+        def stage1(t):
+            a, b = products[2 * t], products[2 * t + 1]
+            nc.scalar.activation(a_win[t][:, S:], a[:], ACT.Square)
+            nc.scalar.activation(b_win[t][:, S:], b[:], ACT.Square)
+            nc.scalar.activation(a_win[t][:, :S], a[:], ACT.Copy, scale=2.0)
+            nc.scalar.activation(b_win[t][:, :S], b[:], ACT.Copy, scale=-1.0)
+            nc.vector.tensor_tensor(p_win[t][:, S:], b[:], rb_t[t][:], MULT)
+            nc.vector.scalar_tensor_tensor(ara[t][:], a[:], 2.0, ra_t[t][:], MULT, MULT)
+            nc.vector.scalar_tensor_tensor(p_win[t][:, :S], a_win[t][:, S:], 0.15, b_win[t][:, S:], ADD, ADD)
+
+        def stage2(t):
+            nc.scalar.activation(pg[t][:], p_win[t][:].indirect(ant_t[:]), ACT.Copy)
+            nc.vector.tensor_tensor(crb[t][:], a_win[t][:].indirect(ant_t[:]), rb_t[t][:], MULT)
+            nc.vector.tensor_tensor(y[t][:], b_win[t][:].indirect(ant_t[:]), ra_t[t][:], MULT)
+            en_turned[t] = bank_tile(2 * t, "en%d" % t)
+            turn_and_add(en_turned[t], [p_win[t][:, :S], pg[t][:]])
+            n1_turned[t] = bank_tile(2 * t + 1, "n1_%d" % t)
+            turn_and_add(n1_turned[t], [p_win[t][:, S:], ara[t][:], crb[t][:]])
+
+        def stage3(t):
+            nc.scalar.activation(rs[t][:], en_turned[t][:], ACT.Abs_reciprocal_sqrt)
+            nc.scalar.activation(inv[t][:], rs[t][:], ACT.Square)
+            nc.vector.tensor_tensor(llr[:, t, :], n1_turned[t][:], rs[t][:], MULT)
+            nc.vector.tensor_tensor(y[t][:], y[t][:], p_win[t][:, S:], ADD)
+
+        def stage4(t):
+            inv_back = bank_tile(2 * t + 1, "inv_back%d" % t)
+            for jb in range(PACK):
+                cols = slice(jb * P, (jb + 1) * P)
+                turn(inv_back, cols, inv[t][:, cols], True, True)
+            nc.vector.scalar_tensor_tensor(s_win[t][:], inv_back[:], unit_t[:, t : t + 1], y[t][:], MULT, MULT)
+            for h in range(2):
+                lst = ant_t[:, h * HALF // 16 : (h + 1) * HALF // 16]
+                nc.scalar.activation(sg[h][:, t, :], s_win[t][:].indirect(lst), ACT.Copy)
+
+        stages = (stage1, stage2, stage3, stage4)
+        for step in range(PACK + len(stages) - 1):
+            for n, stage in enumerate(stages):
+                if 0 <= step - n < PACK:
+                    stage(step - n)
+
+        back = {}
+        for h in range(2):
+            cols = slice(h * HALF, (h + 1) * HALF)
+            th = sb.tile([P, PACK, HALF], F32, name="th%d" % h, align_bytes=64)
+            nc.scalar.activation(th[:], llr[:, :, cols], ACT.Tanh, scale=0.25)
+            for t in range(PACK):
+                nc.vector.tensor_tensor(th[:, t, :], en_turned[t][:, cols], th[:, t, :], MULT)
+                if t % 2 == 0:
+                    bank = bank_tile(4 * h + t + 1, "back%d" % (2 * h + t // 2))
+                back[h, t] = bank[:, (t % 2) * HALF : (t % 2 + 1) * HALF]
+                for jb in range(2):
+                    turn(back[h, t], slice(jb * P, (jb + 1) * P), th[:, t, jb * P : (jb + 1) * P], True, True)
+
+        for h in range(2):
+            cols = slice(h * HALF, (h + 1) * HALF)
+            for t in range(PACK):
+                nc.vector.scalar_tensor_tensor(sg[h][:, t, :], back[h, t], unit_t[:, t : t + 1], sg[h][:, t, :], MULT, ADD)
+            hid = plane("hid%d" % h, PACK * HALF, BF16)
+            nc.vector.tensor_copy(
+                hid[:].rearrange("p (c i t) -> p c t i", i=4, t=PACK),
+                sg[h][:].rearrange("p t (c i) -> p c t i", i=4),
+            )
+            codes = plane("codes%d" % h, HALF, U32)
+            scales = plane("scales%d" % h, HALF, U8)
+            nc.vector.quantize_mx(out=codes[:].bitcast(FP8X4), scales=scales[:], in_=hid[:])
+            acc = bank_tile(4 * h + 1, "acc%d" % h)
+            nc.tensor.matmul_mx(
+                out=acc[:, :HALF],
+                lhsT=w3w[:].bitcast(FP4X4),
+                lhsT_scale=w3s[:],
+                rhs=codes[:].bitcast(FP8X4),
+                rhs_scale=scales[:],
+                start=True,
+                stop=True,
+            )
+            res = plane("res%d" % h, HALF)
+            nc.scalar.activation(res[:], acc[:, :HALF], ACT.Copy)
+            nc.sync.dma_start(out=out[:, cols], in_=res[:])

@@ -20,7 +20,8 @@ ADD = mybir.AluOpType.add
 
 P = 128
 PACK = 4
-HALF = S // 2
+CHUNKS = (256, 128, 128)
+EARLY = 0
 
 
 def load_scale_rows(nc, queue, plane, scales):
@@ -44,8 +45,8 @@ def tile_picked_yalamo_tanh_p_kernel(
         ant_t = sb.tile([P, S // 16], U16, name="ant_t")
         xw = plane("xw", T, U32)
         xs = plane("xs", T, U8)
-        w_raw = [plane("w_raw%d" % i, 2 * H, U8) for i in range(2)]
-        ws_raw = [plane("ws_raw%d" % i, H, U8) for i in range(2)]
+        w_raw = sb.tile([P, 2, 2 * H], U8, name="w_raw", align_bytes=64)
+        ws_raw = sb.tile([P, 2, H], U8, name="ws_raw", tag="ws_raw", align_bytes=64)
         w3w = plane("w3w", 2 * N, U8)
         w3s = plane("w3s", N, U8)
         ra_t = [plane("ra%d" % t) for t in range(PACK)]
@@ -54,40 +55,49 @@ def tile_picked_yalamo_tanh_p_kernel(
 
         ident = plane("ident", P)
 
-        nc.sync.dma_start(out=w_raw[0][:].bitcast(I32), in_=w1_words[0].bitcast(I32))
-        nc.sync.dma_start(out=w_raw[1][:].bitcast(I32), in_=w2_words[0].bitcast(I32))
         nc.sync.dma_start(offs_t[:], offs)
         nc.sync.dma_start(out=xw[:].bitcast(I32), in_=x_words[0].rearrange("p n r -> p (n r)").bitcast(I32))
-        load_scale_rows(nc, nc.sync, xs, x_scales)
-        load_scale_rows(nc, nc.sync, ws_raw[0], w1_scales)
-        load_scale_rows(nc, nc.sync, ws_raw[1], w2_scales)
+        nc.sync.dma_start(out=w_raw[:, 0, :].bitcast(I32), in_=w1_words[0].bitcast(I32))
+        nc.sync.dma_start(out=w_raw[:, 1, :].bitcast(I32), in_=w2_words[0].bitcast(I32))
+        load_scale_rows(nc, nc.scalar, xs[:], x_scales)
+        load_scale_rows(nc, nc.sync, ws_raw[:, 0, :], w1_scales)
+        load_scale_rows(nc, nc.scalar, ws_raw[:, 1, :], w2_scales)
+        warm = plane("warm", 8)
+        nc.gpsimd.memset(warm[:], 1.0)
+        nc.scalar.activation(warm[:], warm[:], ACT.Abs_reciprocal_sqrt)
         make_identity(nc, ident[:])
-        nc.sync.dma_start(ant_t[:], ant)
         ra_v = ra.rearrange("(p t) s -> p t s", t=PACK)
         rb_v = rb.rearrange("(p t) s -> p t s", t=PACK)
         for t in range(PACK):
-            nc.sync.dma_start(out=rb_t[t][:], in_=rb_v[:, t, :])
             nc.sync.dma_start(out=ra_t[t][:], in_=ra_v[:, t, :])
+            nc.sync.dma_start(out=rb_t[t][:], in_=rb_v[:, t, :])
+            if t == 0:
+                nc.sync.dma_start(ant_t[:], ant)
         nc.sync.dma_start(out=unit_t[:], in_=unit.rearrange("(p t) o -> p (t o)", t=PACK))
         nc.sync.dma_start(out=w3w[:].bitcast(I32), in_=w3_words[0].bitcast(I32))
-        load_scale_rows(nc, nc.sync, w3s, w3_scales)
+        load_scale_rows(nc, nc.sync, w3s[:], w3_scales)
 
-        w_dealt = [plane("w_dealt%d" % i, 2 * H, U8) for i in range(2)]
-        ws_dealt = [plane("ws_dealt%d" % i, H, U8) for i in range(2)]
+        w_dealt = {}
+        ws_dealt = {}
         xg = plane("xg", S, U32)
         xsg = plane("xsg", S, U8)
-        for i in range(2):
+
+        def deal(dealt, raw, first, last, size, name, tag):
+            made = sb.tile([P, 2, last - first, P * size], U8, name=name, tag=tag, align_bytes=64)
             nc.vector.tensor_copy(
-                w_dealt[i][:].rearrange("p (t m b) -> p t m b", t=PACK, b=2),
-                w_raw[i][:].rearrange("p (m t b) -> p t m b", t=PACK, b=2),
+                made[:].rearrange("p i t (m b) -> p i t m b", b=size),
+                raw[:].rearrange("p i (m t b) -> p i t m b", t=PACK, b=size)[:, :, first:last],
             )
+            for i in range(2):
+                for t in range(first, last):
+                    dealt[i, t] = made[:, i, t - first, :]
+
         nc.vector.tensor_copy(xg[:], xw[:].indirect(offs_t[:]))
+        deal(w_dealt, w_raw, 0, 1, 2, "w_first", "w_first")
         nc.vector.tensor_copy(xsg[:], xs[:].indirect(offs_t[:]))
-        for i in range(2):
-            nc.vector.tensor_copy(
-                ws_dealt[i][:].rearrange("p (t m) -> p t m", t=PACK),
-                ws_raw[i][:].rearrange("p (m t) -> p t m", t=PACK),
-            )
+        deal(ws_dealt, ws_raw, 0, 1, 1, "ws_first", "ws_first")
+        deal(ws_dealt, ws_raw, 1, PACK, 1, "ws_last", "ws_last")
+        deal(w_dealt, w_raw, 1, PACK, 2, "w_last", "ws_raw")
 
         def bank_tile(index, name):
             return psum.tile([P, S], F32, name=name, tag="bank%d" % index)
@@ -112,7 +122,6 @@ def tile_picked_yalamo_tanh_p_kernel(
         rs = [plane("rs%d" % t) for t in range(PACK)]
         inv = [plane("inv%d" % t) for t in range(PACK)]
         llr = sb.tile([P, PACK, S], F32, name="llr", align_bytes=64)
-        sg = [sb.tile([P, PACK, HALF], F32, name="sg%d" % h, align_bytes=64) for h in range(2)]
 
         products = []
         for t in range(PACK):
@@ -120,8 +129,8 @@ def tile_picked_yalamo_tanh_p_kernel(
                 bank = bank_tile(2 * t + i, "prod%d" % (2 * t + i))
                 nc.tensor.matmul_mx(
                     out=bank[:],
-                    lhsT=w_dealt[i][:, 2 * P * t : 2 * P * (t + 1)].bitcast(FP4X4),
-                    lhsT_scale=ws_dealt[i][:, P * t : P * (t + 1)],
+                    lhsT=w_dealt[i, t].bitcast(FP4X4),
+                    lhsT_scale=ws_dealt[i, t],
                     rhs=xg[:].bitcast(FP8X4),
                     rhs_scale=xsg[:],
                     start=True,
@@ -132,75 +141,100 @@ def tile_picked_yalamo_tanh_p_kernel(
         en_turned = {}
         n1_turned = {}
 
-        def stage1(t):
+        chunks = [(sum(CHUNKS[:c]), width) for c, width in enumerate(CHUNKS)]
+        sg = [sb.tile([P, PACK, width], F32, name="sg%d" % c, align_bytes=64) for c, width in enumerate(CHUNKS)]
+
+        def own_terms(t):
             a, b = products[2 * t], products[2 * t + 1]
-            nc.scalar.activation(a_win[t][:, S:], a[:], ACT.Square)
-            nc.scalar.activation(b_win[t][:, S:], b[:], ACT.Square)
+            nc.vector.scalar_tensor_tensor(ara[t][:], a[:], 2.0, ra_t[t][:], MULT, MULT)
+            nc.vector.tensor_tensor(b_win[t][:, S:], b[:], rb_t[t][:], MULT)
+
+        def empty_products(t):
+            a, b = products[2 * t], products[2 * t + 1]
+            nc.scalar.activation(p_win[t][:, S:], a[:], ACT.Square)
+            nc.scalar.activation(a_win[t][:, S:], b[:], ACT.Square)
             nc.scalar.activation(a_win[t][:, :S], a[:], ACT.Copy, scale=2.0)
             nc.scalar.activation(b_win[t][:, :S], b[:], ACT.Copy, scale=-1.0)
-            nc.vector.tensor_tensor(p_win[t][:, S:], b[:], rb_t[t][:], MULT)
-            nc.vector.scalar_tensor_tensor(ara[t][:], a[:], 2.0, ra_t[t][:], MULT, MULT)
-            nc.vector.scalar_tensor_tensor(p_win[t][:, :S], a_win[t][:, S:], 0.15, b_win[t][:, S:], ADD, ADD)
+            nc.vector.scalar_tensor_tensor(p_win[t][:, :S], p_win[t][:, S:], 0.15, a_win[t][:, S:], ADD, ADD)
 
-        def stage2(t):
+        def sums(t):
             nc.scalar.activation(pg[t][:], p_win[t][:].indirect(ant_t[:]), ACT.Copy)
             nc.vector.tensor_tensor(crb[t][:], a_win[t][:].indirect(ant_t[:]), rb_t[t][:], MULT)
-            nc.vector.tensor_tensor(y[t][:], b_win[t][:].indirect(ant_t[:]), ra_t[t][:], MULT)
             en_turned[t] = bank_tile(2 * t, "en%d" % t)
             turn_and_add(en_turned[t], [p_win[t][:, :S], pg[t][:]])
             n1_turned[t] = bank_tile(2 * t + 1, "n1_%d" % t)
-            turn_and_add(n1_turned[t], [p_win[t][:, S:], ara[t][:], crb[t][:]])
+            turn_and_add(n1_turned[t], [b_win[t][:, S:], ara[t][:], crb[t][:]])
 
-        def stage3(t):
+        def root(t):
             nc.scalar.activation(rs[t][:], en_turned[t][:], ACT.Abs_reciprocal_sqrt)
-            nc.scalar.activation(inv[t][:], rs[t][:], ACT.Square)
             nc.vector.tensor_tensor(llr[:, t, :], n1_turned[t][:], rs[t][:], MULT)
-            nc.vector.tensor_tensor(y[t][:], y[t][:], p_win[t][:, S:], ADD)
 
-        def stage4(t):
+        def second_numerator(t):
+            if t < 2:
+                nc.scalar.activation(y[t][:], b_win[t][:].indirect(ant_t[:]), ACT.Copy)
+                nc.vector.tensor_tensor(y[t][:], y[t][:], ra_t[t][:], MULT)
+            else:
+                nc.vector.tensor_tensor(y[t][:], b_win[t][:].indirect(ant_t[:]), ra_t[t][:], MULT)
+
+        def second_symbol(t):
+            nc.scalar.activation(inv[t][:], rs[t][:], ACT.Square)
             inv_back = bank_tile(2 * t + 1, "inv_back%d" % t)
             for jb in range(PACK):
                 cols = slice(jb * P, (jb + 1) * P)
                 turn(inv_back, cols, inv[t][:, cols], True, True)
+            nc.vector.tensor_tensor(y[t][:], y[t][:], b_win[t][:, S:], ADD)
             nc.vector.scalar_tensor_tensor(s_win[t][:], inv_back[:], unit_t[:, t : t + 1], y[t][:], MULT, MULT)
-            for h in range(2):
-                lst = ant_t[:, h * HALF // 16 : (h + 1) * HALF // 16]
-                nc.scalar.activation(sg[h][:, t, :], s_win[t][:].indirect(lst), ACT.Copy)
 
-        stages = (stage1, stage2, stage3, stage4)
-        for step in range(PACK + len(stages) - 1):
-            for n, stage in enumerate(stages):
-                if 0 <= step - n < PACK:
-                    stage(step - n)
+        def fetch_symbol(t, c):
+            first, width = chunks[c]
+            picked = s_win[t][:].indirect(ant_t[:, first // 16 : (first + width) // 16])
+            nc.scalar.activation(sg[c][:, t, :], picked, ACT.Copy)
+
+        def fetch_early(t):
+            if t < EARLY:
+                for c in range(len(chunks)):
+                    fetch_symbol(t, c)
+
+        stages = ((own_terms, 0), (empty_products, 0), (root, 1), (sums, 0), (second_numerator, 3), (second_symbol, 4), (fetch_early, 5))
+        for step in range(PACK + max(lag for stage, lag in stages)):
+            for stage, lag in stages:
+                if 0 <= step - lag < PACK:
+                    stage(step - lag)
 
         back = {}
-        for h in range(2):
-            cols = slice(h * HALF, (h + 1) * HALF)
-            th = sb.tile([P, PACK, HALF], F32, name="th%d" % h, align_bytes=64)
+        for c, (first, width) in enumerate(chunks):
+            cols = slice(first, first + width)
+            th = sb.tile([P, PACK, width], F32, name="th%d" % c, align_bytes=64)
             nc.scalar.activation(th[:], llr[:, :, cols], ACT.Tanh, scale=0.25)
             for t in range(PACK):
                 nc.vector.tensor_tensor(th[:, t, :], en_turned[t][:, cols], th[:, t, :], MULT)
-                if t % 2 == 0:
-                    bank = bank_tile(4 * h + t + 1, "back%d" % (2 * h + t // 2))
-                back[h, t] = bank[:, (t % 2) * HALF : (t % 2 + 1) * HALF]
-                for jb in range(2):
-                    turn(back[h, t], slice(jb * P, (jb + 1) * P), th[:, t, jb * P : (jb + 1) * P], True, True)
+                at = PACK * first + t * width
+                if at % S == 0:
+                    bank = bank_tile(2 * (at // S) + 1, "back%d" % (at // S))
+                back[c, t] = bank[:, at % S : at % S + width]
+                for jb in range(width // P):
+                    block = slice(jb * P, (jb + 1) * P)
+                    turn(back[c, t], block, th[:, t, block], True, True)
 
-        for h in range(2):
-            cols = slice(h * HALF, (h + 1) * HALF)
+        for c in range(len(chunks)):
+            for t in range(EARLY, PACK):
+                fetch_symbol(t, c)
+
+        for c, (first, width) in enumerate(chunks):
             for t in range(PACK):
-                nc.vector.scalar_tensor_tensor(sg[h][:, t, :], back[h, t], unit_t[:, t : t + 1], sg[h][:, t, :], MULT, ADD)
-            hid = plane("hid%d" % h, PACK * HALF, BF16)
-            nc.vector.tensor_copy(
+                nc.vector.scalar_tensor_tensor(sg[c][:, t, :], back[c, t], unit_t[:, t : t + 1], sg[c][:, t, :], MULT, ADD)
+            hid = plane("hid%d" % c, PACK * width, BF16)
+            weave = nc.vector.tensor_copy if c >= 0 else nc.scalar.copy
+            weave(
                 hid[:].rearrange("p (c i t) -> p c t i", i=4, t=PACK),
-                sg[h][:].rearrange("p t (c i) -> p c t i", i=4),
+                sg[c][:].rearrange("p t (c i) -> p c t i", i=4),
             )
-            codes = plane("codes%d" % h, HALF, U32)
-            scales = plane("scales%d" % h, HALF, U8)
+            codes = plane("codes%d" % c, width, U32)
+            scales = plane("scales%d" % c, width, U8)
             nc.vector.quantize_mx(out=codes[:].bitcast(FP8X4), scales=scales[:], in_=hid[:])
-            acc = bank_tile(4 * h + 1, "acc%d" % h)
+            acc = bank_tile(2 * (PACK * first // S) + 1, "acc%d" % c)
             nc.tensor.matmul_mx(
-                out=acc[:, :HALF],
+                out=acc[:, :width],
                 lhsT=w3w[:].bitcast(FP4X4),
                 lhsT_scale=w3s[:],
                 rhs=codes[:].bitcast(FP8X4),
@@ -208,6 +242,6 @@ def tile_picked_yalamo_tanh_p_kernel(
                 start=True,
                 stop=True,
             )
-            res = plane("res%d" % h, HALF)
-            nc.scalar.activation(res[:], acc[:, :HALF], ACT.Copy)
-            nc.sync.dma_start(out=out[:, cols], in_=res[:])
+            res = plane("res%d" % c, width)
+            nc.scalar.activation(res[:], acc[:, :width], ACT.Copy)
+            nc.sync.dma_start(out=out[:, first : first + width], in_=res[:])

@@ -27,7 +27,7 @@ EARLY = 0
 def load_scale_rows(nc, queue, plane, scales):
     for q in range(4):
         rows = scales[0, 4 * q : 4 * q + 4, :].bitcast(I32)
-        queue.dma_start(out=plane[32 * q : 32 * q + 32, :].bitcast(I32), in_=rows.partition_broadcast(8))
+        queue.dma_start(out=plane[32 * q : 32 * q + 4, :].bitcast(I32), in_=rows)
 
 
 def tile_picked_yalamo_tanh_p_kernel(
@@ -55,6 +55,8 @@ def tile_picked_yalamo_tanh_p_kernel(
 
         ident = plane("ident", P)
 
+        nc.gpsimd.memset(xs[:].bitcast(I32), 0)
+        nc.gpsimd.memset(ws_raw[:].bitcast(I32), 0)
         nc.sync.dma_start(offs_t[:], offs)
         nc.sync.dma_start(out=xw[:].bitcast(I32), in_=x_words[0].rearrange("p n r -> p (n r)").bitcast(I32))
         nc.sync.dma_start(out=w_raw[:, 0, :].bitcast(I32), in_=w1_words[0].bitcast(I32))
@@ -66,6 +68,7 @@ def tile_picked_yalamo_tanh_p_kernel(
         nc.gpsimd.memset(warm[:], 1.0)
         nc.scalar.activation(warm[:], warm[:], ACT.Abs_reciprocal_sqrt)
         make_identity(nc, ident[:])
+        nc.gpsimd.memset(w3s[:].bitcast(I32), 0)
         ra_v = ra.rearrange("(p t) s -> p t s", t=PACK)
         rb_v = rb.rearrange("(p t) s -> p t s", t=PACK)
         for t in range(PACK):
@@ -149,10 +152,17 @@ def tile_picked_yalamo_tanh_p_kernel(
             nc.vector.scalar_tensor_tensor(ara[t][:], a[:], 2.0, ra_t[t][:], MULT, MULT)
             nc.vector.tensor_tensor(b_win[t][:, S:], b[:], rb_t[t][:], MULT)
 
-        def empty_products(t):
+        def squares(t):
             a, b = products[2 * t], products[2 * t + 1]
             nc.scalar.activation(p_win[t][:, S:], a[:], ACT.Square)
             nc.scalar.activation(a_win[t][:, S:], b[:], ACT.Square)
+
+        def read_products(t):
+            for reader in (squares, own_terms) if t == 0 else (own_terms, squares):
+                reader(t)
+
+        def empty_products(t):
+            a, b = products[2 * t], products[2 * t + 1]
             nc.scalar.activation(a_win[t][:, :S], a[:], ACT.Copy, scale=2.0)
             nc.scalar.activation(b_win[t][:, :S], b[:], ACT.Copy, scale=-1.0)
             nc.vector.scalar_tensor_tensor(p_win[t][:, :S], p_win[t][:, S:], 0.15, a_win[t][:, S:], ADD, ADD)
@@ -170,11 +180,7 @@ def tile_picked_yalamo_tanh_p_kernel(
             nc.vector.tensor_tensor(llr[:, t, :], n1_turned[t][:], rs[t][:], MULT)
 
         def second_numerator(t):
-            if t < 2:
-                nc.scalar.activation(y[t][:], b_win[t][:].indirect(ant_t[:]), ACT.Copy)
-                nc.vector.tensor_tensor(y[t][:], y[t][:], ra_t[t][:], MULT)
-            else:
-                nc.vector.tensor_tensor(y[t][:], b_win[t][:].indirect(ant_t[:]), ra_t[t][:], MULT)
+            nc.vector.tensor_tensor(y[t][:], b_win[t][:].indirect(ant_t[:]), ra_t[t][:], MULT)
 
         def second_symbol(t):
             nc.scalar.activation(inv[t][:], rs[t][:], ACT.Square)
@@ -195,7 +201,7 @@ def tile_picked_yalamo_tanh_p_kernel(
                 for c in range(len(chunks)):
                     fetch_symbol(t, c)
 
-        stages = ((own_terms, 0), (empty_products, 0), (root, 1), (sums, 0), (second_numerator, 3), (second_symbol, 4), (fetch_early, 5))
+        stages = ((read_products, 0), (empty_products, 0), (root, 2), (sums, 1), (second_numerator, 5), (second_symbol, 5), (fetch_early, 6))
         for step in range(PACK + max(lag for stage, lag in stages)):
             for stage, lag in stages:
                 if 0 <= step - lag < PACK:

from contextlib import ExitStack

import concourse.mybir as mybir
from concourse.masks import make_identity

K, T, S, N, H = 512, 1024, 512, 128, 512
FLOPS = 2 * K * S * H * 2 + 2 * H * S * N

F32 = mybir.dt.float32
BF16 = mybir.dt.bfloat16
I32 = mybir.dt.int32
U32 = mybir.dt.uint32
U16 = mybir.dt.uint16
U8 = mybir.dt.uint8
FP8X4 = mybir.dt.float8_e4m3fn_x4
FP4X4 = mybir.dt.float4_e2m1fn_x4
ACT = mybir.ActivationFunctionType
MULT = mybir.AluOpType.mult
ADD = mybir.AluOpType.add

P = 128
PACK = 4
CHUNKS = (256, 128, 128)
EARLY = 0


def load_scale_rows(nc, queue, plane, scales):
    for q in range(4):
        rows = scales[0, 4 * q : 4 * q + 4, :].bitcast(I32)
        queue.dma_start(out=plane[32 * q : 32 * q + 4, :].bitcast(I32), in_=rows)


def tile_picked_yalamo_tanh_p_kernel(
    tc, x_words, x_scales, w1_words, w1_scales, w2_words, w2_scales, ra, rb, unit, w3_words, w3_scales, offs, ant, out
):
    nc = tc.nc
    with ExitStack() as ctx:
        sb = ctx.enter_context(tc.tile_pool(name="sb", bufs=1))
        psum = ctx.enter_context(tc.psum_pool(name="psum", bufs=1))

        def plane(name, width=S, dtype=F32):
            return sb.tile([P, width], dtype, name=name, align_bytes=64)

        offs_t = sb.tile([P, S // 16], U16, name="offs_t")
        ant_t = sb.tile([P, S // 16], U16, name="ant_t")
        xw = plane("xw", T, U32)
        xs = plane("xs", T, U8)
        w_raw = sb.tile([P, 2, 2 * H], U8, name="w_raw", align_bytes=64)
        ws_raw = sb.tile([P, 2, H], U8, name="ws_raw", tag="ws_raw", align_bytes=64)
        w3w = plane("w3w", 2 * N, U8)
        w3s = plane("w3s", N, U8)
        ra_t = [plane("ra%d" % t) for t in range(PACK)]
        rb_t = [plane("rb%d" % t) for t in range(PACK)]
        unit_t = plane("unit_t", PACK)

        ident = plane("ident", P)

        nc.gpsimd.memset(xs[:].bitcast(I32), 0)
        nc.gpsimd.memset(ws_raw[:].bitcast(I32), 0)
        nc.sync.dma_start(offs_t[:], offs)
        nc.sync.dma_start(out=xw[:].bitcast(I32), in_=x_words[0].rearrange("p n r -> p (n r)").bitcast(I32))
        nc.sync.dma_start(out=w_raw[:, 0, :].bitcast(I32), in_=w1_words[0].bitcast(I32))
        nc.sync.dma_start(out=w_raw[:, 1, :].bitcast(I32), in_=w2_words[0].bitcast(I32))
        load_scale_rows(nc, nc.scalar, xs[:], x_scales)
        load_scale_rows(nc, nc.sync, ws_raw[:, 0, :], w1_scales)
        load_scale_rows(nc, nc.scalar, ws_raw[:, 1, :], w2_scales)
        warm = plane("warm", 8)
        nc.gpsimd.memset(warm[:], 1.0)
        nc.scalar.activation(warm[:], warm[:], ACT.Abs_reciprocal_sqrt)
        make_identity(nc, ident[:])
        nc.gpsimd.memset(w3s[:].bitcast(I32), 0)
        ra_v = ra.rearrange("(p t) s -> p t s", t=PACK)
        rb_v = rb.rearrange("(p t) s -> p t s", t=PACK)
        for t in range(PACK):
            nc.sync.dma_start(out=ra_t[t][:], in_=ra_v[:, t, :])
            nc.sync.dma_start(out=rb_t[t][:], in_=rb_v[:, t, :])
            if t == 0:
                nc.sync.dma_start(ant_t[:], ant)
        nc.sync.dma_start(out=unit_t[:], in_=unit.rearrange("(p t) o -> p (t o)", t=PACK))
        nc.sync.dma_start(out=w3w[:].bitcast(I32), in_=w3_words[0].bitcast(I32))
        load_scale_rows(nc, nc.sync, w3s[:], w3_scales)

        w_dealt = {}
        ws_dealt = {}
        xg = plane("xg", S, U32)
        xsg = plane("xsg", S, U8)

        def deal(dealt, raw, first, last, size, name, tag):
            made = sb.tile([P, 2, last - first, P * size], U8, name=name, tag=tag, align_bytes=64)
            nc.vector.tensor_copy(
                made[:].rearrange("p i t (m b) -> p i t m b", b=size),
                raw[:].rearrange("p i (m t b) -> p i t m b", t=PACK, b=size)[:, :, first:last],
            )
            for i in range(2):
                for t in range(first, last):
                    dealt[i, t] = made[:, i, t - first, :]

        nc.vector.tensor_copy(xg[:], xw[:].indirect(offs_t[:]))
        deal(w_dealt, w_raw, 0, 1, 2, "w_first", "w_first")
        nc.vector.tensor_copy(xsg[:], xs[:].indirect(offs_t[:]))
        deal(ws_dealt, ws_raw, 0, 1, 1, "ws_first", "ws_first")
        deal(ws_dealt, ws_raw, 1, PACK, 1, "ws_last", "ws_last")
        deal(w_dealt, w_raw, 1, PACK, 2, "w_last", "ws_raw")

        def bank_tile(index, name):
            return psum.tile([P, S], F32, name=name, tag="bank%d" % index)

        def turn(bank, cols, src, start, stop):
            nc.tensor.matmul(bank[:, cols], src, ident[:], start=start, stop=stop, is_transpose=True)

        def turn_and_add(bank, terms):
            for n, term in enumerate(terms):
                for jb in range(PACK):
                    cols = slice(jb * P, (jb + 1) * P)
                    turn(bank, cols, term[:, cols], n == 0 and jb == 0, n == len(terms) - 1 and jb == PACK - 1)

        a_win = [plane("a_win%d" % t, 2 * S) for t in range(PACK)]
        b_win = [plane("b_win%d" % t, 2 * S) for t in range(PACK)]
        p_win = [plane("p_win%d" % t, 2 * S) for t in range(PACK)]
        s_win = [plane("s_win%d" % t) for t in range(PACK)]
        ara = [plane("ara%d" % t) for t in range(PACK)]
        crb = [plane("crb%d" % t) for t in range(PACK)]
        pg = [plane("pg%d" % t) for t in range(PACK)]
        y = [plane("y%d" % t) for t in range(PACK)]
        rs = [plane("rs%d" % t) for t in range(PACK)]
        inv = [plane("inv%d" % t) for t in range(PACK)]
        llr = sb.tile([P, PACK, S], F32, name="llr", align_bytes=64)

        products = []
        for t in range(PACK):
            for i in range(2):
                bank = bank_tile(2 * t + i, "prod%d" % (2 * t + i))
                nc.tensor.matmul_mx(
                    out=bank[:],
                    lhsT=w_dealt[i, t].bitcast(FP4X4),
                    lhsT_scale=ws_dealt[i, t],
                    rhs=xg[:].bitcast(FP8X4),
                    rhs_scale=xsg[:],
                    start=True,
                    stop=True,
                )
                products.append(bank)

        en_turned = {}
        n1_turned = {}

        chunks = [(sum(CHUNKS[:c]), width) for c, width in enumerate(CHUNKS)]
        sg = [sb.tile([P, PACK, width], F32, name="sg%d" % c, align_bytes=64) for c, width in enumerate(CHUNKS)]

        def own_terms(t):
            a, b = products[2 * t], products[2 * t + 1]
            nc.vector.scalar_tensor_tensor(ara[t][:], a[:], 2.0, ra_t[t][:], MULT, MULT)
            nc.vector.tensor_tensor(b_win[t][:, S:], b[:], rb_t[t][:], MULT)

        def squares(t):
            a, b = products[2 * t], products[2 * t + 1]
            nc.scalar.activation(p_win[t][:, S:], a[:], ACT.Square)
            nc.scalar.activation(a_win[t][:, S:], b[:], ACT.Square)

        def read_products(t):
            for reader in (squares, own_terms) if t == 0 else (own_terms, squares):
                reader(t)

        def empty_products(t):
            a, b = products[2 * t], products[2 * t + 1]
            nc.scalar.activation(a_win[t][:, :S], a[:], ACT.Copy, scale=2.0)
            nc.scalar.activation(b_win[t][:, :S], b[:], ACT.Copy, scale=-1.0)
            nc.vector.scalar_tensor_tensor(p_win[t][:, :S], p_win[t][:, S:], 0.15, a_win[t][:, S:], ADD, ADD)

        def sums(t):
            nc.scalar.activation(pg[t][:], p_win[t][:].indirect(ant_t[:]), ACT.Copy)
            nc.vector.tensor_tensor(crb[t][:], a_win[t][:].indirect(ant_t[:]), rb_t[t][:], MULT)
            en_turned[t] = bank_tile(2 * t, "en%d" % t)
            turn_and_add(en_turned[t], [p_win[t][:, :S], pg[t][:]])
            n1_turned[t] = bank_tile(2 * t + 1, "n1_%d" % t)
            turn_and_add(n1_turned[t], [b_win[t][:, S:], ara[t][:], crb[t][:]])

        def root(t):
            nc.scalar.activation(rs[t][:], en_turned[t][:], ACT.Abs_reciprocal_sqrt)
            nc.vector.tensor_tensor(llr[:, t, :], n1_turned[t][:], rs[t][:], MULT)

        def second_numerator(t):
            nc.vector.tensor_tensor(y[t][:], b_win[t][:].indirect(ant_t[:]), ra_t[t][:], MULT)

        def second_symbol(t):
            nc.scalar.activation(inv[t][:], rs[t][:], ACT.Square)
            inv_back = bank_tile(2 * t + 1, "inv_back%d" % t)
            for jb in range(PACK):
                cols = slice(jb * P, (jb + 1) * P)
                turn(inv_back, cols, inv[t][:, cols], True, True)
            nc.vector.tensor_tensor(y[t][:], y[t][:], b_win[t][:, S:], ADD)
            nc.vector.scalar_tensor_tensor(s_win[t][:], inv_back[:], unit_t[:, t : t + 1], y[t][:], MULT, MULT)

        def fetch_symbol(t, c):
            first, width = chunks[c]
            picked = s_win[t][:].indirect(ant_t[:, first // 16 : (first + width) // 16])
            nc.scalar.activation(sg[c][:, t, :], picked, ACT.Copy)

        def fetch_early(t):
            if t < EARLY:
                for c in range(len(chunks)):
                    fetch_symbol(t, c)

        stages = ((read_products, 0), (empty_products, 0), (root, 2), (sums, 1), (second_numerator, 5), (second_symbol, 5), (fetch_early, 6))
        for step in range(PACK + max(lag for stage, lag in stages)):
            for stage, lag in stages:
                if 0 <= step - lag < PACK:
                    stage(step - lag)

        back = {}
        for c, (first, width) in enumerate(chunks):
            cols = slice(first, first + width)
            th = sb.tile([P, PACK, width], F32, name="th%d" % c, align_bytes=64)
            nc.scalar.activation(th[:], llr[:, :, cols], ACT.Tanh, scale=0.25)
            for t in range(PACK):
                nc.vector.tensor_tensor(th[:, t, :], en_turned[t][:, cols], th[:, t, :], MULT)
                at = PACK * first + t * width
                if at % S == 0:
                    bank = bank_tile(2 * (at // S) + 1, "back%d" % (at // S))
                back[c, t] = bank[:, at % S : at % S + width]
                for jb in range(width // P):
                    block = slice(jb * P, (jb + 1) * P)
                    turn(back[c, t], block, th[:, t, block], True, True)

        for c in range(len(chunks)):
            for t in range(EARLY, PACK):
                fetch_symbol(t, c)

        for c, (first, width) in enumerate(chunks):
            for t in range(PACK):
                nc.vector.scalar_tensor_tensor(sg[c][:, t, :], back[c, t], unit_t[:, t : t + 1], sg[c][:, t, :], MULT, ADD)
            hid = plane("hid%d" % c, PACK * width, BF16)
            weave = nc.vector.tensor_copy if c >= 0 else nc.scalar.copy
            weave(
                hid[:].rearrange("p (c i t) -> p c t i", i=4, t=PACK),
                sg[c][:].rearrange("p t (c i) -> p c t i", i=4),
            )
            codes = plane("codes%d" % c, width, U32)
            scales = plane("scales%d" % c, width, U8)
            nc.vector.quantize_mx(out=codes[:].bitcast(FP8X4), scales=scales[:], in_=hid[:])
            acc = bank_tile(2 * (PACK * first // S) + 1, "acc%d" % c)
            nc.tensor.matmul_mx(
                out=acc[:, :width],
                lhsT=w3w[:].bitcast(FP4X4),
                lhsT_scale=w3s[:],
                rhs=codes[:].bitcast(FP8X4),
                rhs_scale=scales[:],
                start=True,
                stop=True,
            )
            res = plane("res%d" % c, width)
            nc.scalar.activation(res[:], acc[:, :width], ACT.Copy)
            nc.sync.dma_start(out=out[:, first : first + width], in_=res[:])
